import numpy as np
import ml_dtypes


def mxq(x, axis, fmt="e4m3"):
    dtype, down = {"e4m3": (ml_dtypes.float8_e4m3fn, 7), "e5m2": (ml_dtypes.float8_e5m2, 14)}[fmt]
    v = np.moveaxis(np.asarray(x, np.float32).astype(ml_dtypes.bfloat16).astype(np.float64), axis, -1)
    blocks = v.reshape(v.shape[:-1] + (-1, 32))
    amax = np.abs(blocks).max(-1, keepdims=True)
    byte = np.maximum(np.where(amax > 0, np.frexp(amax)[1] - 1 + 127, 0) - down, 1)
    scale = np.exp2(byte - 127.0)
    codes = (blocks / scale).astype(np.float32).astype(dtype).astype(np.float64)
    return np.moveaxis((codes * scale).reshape(v.shape), -1, axis)


WIDE = False


def mx_kscale(k):
    if not WIDE:
        return np.ones(k)
    levels = np.array([10, -10, 5, -5, 0])
    if k % 512:
        return np.exp2(np.random.permutation(np.resize(levels, k // 32))).repeat(32)
    a = np.empty((k // 512, 16))
    for p in range(k // 512):
        a[p, :8] = np.random.permutation(np.resize(levels, 8))
        for g in range(8):
            far = levels[np.abs(levels - a[p, g]) >= 10]
            a[p, g + 8] = far[np.random.randint(len(far))]
    return np.exp2(a.ravel()).repeat(32)


def f64(x):
    return np.asarray(x).astype(np.float64)


def striped8(idx):
    return np.asarray(idx).reshape(8, -1, 16).transpose(0, 2, 1).reshape(128, -1).astype(np.uint16)


def unstriped8(offs):
    return offs.reshape(8, 16, -1).transpose(0, 2, 1).reshape(8, -1).astype(np.int64)


def pick8(x, idx, run):
    r = np.arange(len(x))
    return x[r[:, None], idx[r % (8 * run) // run]]


E2M1 = np.array([0.0, 0.5, 1.0, 1.5, 2.0, 3.0, 4.0, 6.0, -0.0, -0.5, -1.0, -1.5, -2.0, -3.0, -4.0, -6.0])


def pack_weight(w, fmt):
    k, n = w.shape
    w = f64(np.asarray(w, np.float32).astype(ml_dtypes.bfloat16)).reshape(k // 32, 32, n)
    amax = np.abs(w).max(1)
    if fmt == "e4m3":
        byte = np.frexp(amax)[1] - 1 + 127 - 7
    else:
        mant, ex = np.frexp(amax / 6.0)
        byte = np.where(mant > 0.5, ex, ex - 1) + 127
    byte = np.clip(np.where(amax > 0, byte, 1), 1, 254)
    scaled = (w * np.exp2(127.0 - byte)[:, None, :]).reshape(k, n).astype(np.float32)
    by_word = np.ascontiguousarray(scaled.reshape(k // 512, 128, 4, n).transpose(0, 1, 3, 2))
    if fmt == "e4m3":
        words = by_word.astype(ml_dtypes.float8_e4m3fn).view(np.uint8)
    else:
        c = by_word.astype(ml_dtypes.float4_e2m1fn).view(np.uint8) & 0xF
        words = (c[..., 0::2] | (c[..., 1::2] << 4)).reshape(k // 512, 128, 2 * n)
    return np.ascontiguousarray(words), np.ascontiguousarray(byte.astype(np.uint8).reshape(k // 512, 16, n))


def unpack_weight(words, scales, fmt):
    g, _, n = scales.shape
    words = np.ascontiguousarray(words).reshape(g, 128, n, -1)
    if fmt == "e4m3":
        vals = words.view(ml_dtypes.float8_e4m3fn).astype(np.float64)
    else:
        nib = np.empty((g, 128, n, 4), np.uint8)
        nib[..., 0::2] = words & 0xF
        nib[..., 1::2] = words >> 4
        vals = E2M1[nib]
    vals = vals * np.repeat(np.exp2(scales.astype(np.float64) - 127.0), 8, axis=1)[..., None]
    return vals.transpose(0, 1, 3, 2).reshape(g * 512, n)


D, T, U, I, J, Q, E = 512, 1024, 1024, 512, 256, 512, 256


def setup_inputs():
    n = np.random.standard_normal
    idx = np.stack([np.random.permutation(T)[:I] for _ in range(8)])
    idx2 = np.stack([np.random.permutation(U)[:I] for _ in range(8)])
    idx3 = np.stack([np.random.permutation(I)[:J] for _ in range(8)])
    idx4 = np.stack([np.random.permutation(T)[:J] for _ in range(8)])
    idx5 = np.stack([np.random.permutation(T)[:I] for _ in range(8)])
    fd = mx_kscale(D)
    fq = mx_kscale(Q)
    keysp = pack_weight(n((D, T)) / fd[:, None], "e2m1")
    notesp = pack_weight(n((D, U)) / fd[:, None], "e4m3")
    mixp = pack_weight(n((Q, E)) * 1.0 / np.sqrt(Q) / fq[:, None], "e4m3")
    return {
        "query": (n((D, Q)) * 1.0 / np.sqrt(D) * fd[:, None]).astype(np.float32),
        "query2": (n((D, Q)) * 1.0 / np.sqrt(D) * fd[:, None]).astype(np.float32),
        "keys_words": keysp[0],
        "keys_scales": keysp[1],
        "notes_words": notesp[0],
        "notes_scales": notesp[1],
        "rowf": (np.random.uniform(0.5, 2.0, (Q, 1)) * fq[:, None]).astype(np.float32),
        "mix_words": mixp[0],
        "mix_scales": mixp[1],
        "offs": striped8(idx),
        "offs2": striped8(idx2),
        "offs3": striped8(idx3),
        "offs4": striped8(idx4),
        "offs5": striped8(idx5),
    }


def reference(query, query2, keys_words, keys_scales, notes_words, notes_scales, rowf, mix_words, mix_scales, offs, offs2, offs3, offs4, offs5):
    idx = unstriped8(offs)
    idx2 = unstriped8(offs2)
    idx3 = unstriped8(offs3)
    idx4 = unstriped8(offs4)
    idx5 = unstriped8(offs5)
    keysu = unpack_weight(keys_words, keys_scales, "e2m1")
    notesu = unpack_weight(notes_words, notes_scales, "e4m3")
    mixu = unpack_weight(mix_words, mix_scales, "e4m3")
    queryq = mxq(f64(query), 0, "e4m3")
    a = queryq.T @ keysu
    query2q = mxq(f64(query2), 0, "e4m3")
    b = query2q.T @ notesu
    r = pick8(a, idx, 64) - pick8(b, idx2, 64)
    w = pick8(r, idx3, 64) * 2.0
    f1 = np.zeros((Q, T))
    f1[np.arange(Q)[:, None], idx4[np.arange(Q) % 512 // 64]] = w
    cc = a + f1
    g = pick8(cc, idx5, 64)
    gw = g * f64(rowf)
    gwq = mxq(gw, 0, "e4m3")
    y = mixu.T @ gwq
    return y

@@ -1,0 +1,266 @@
+from contextlib import ExitStack
+
+import concourse.mybir as mybir
+
+D, T, U, I, J, Q, E = 512, 1024, 1024, 512, 256, 512, 256
+FLOPS = 2 * D * Q * T + 2 * D * Q * U + 2 * Q * E * I
+
+F32 = mybir.dt.float32
+BF16 = mybir.dt.bfloat16
+I32 = mybir.dt.int32
+U32 = mybir.dt.uint32
+U16 = mybir.dt.uint16
+U8 = mybir.dt.uint8
+FP8X4 = mybir.dt.float8_e4m3fn_x4
+FP4X4 = mybir.dt.float4_e2m1fn_x4
+ADD = mybir.AluOpType.add
+SUB = mybir.AluOpType.subtract
+MULT = mybir.AluOpType.mult
+COPY = mybir.ActivationFunctionType.Copy
+
+P = 128
+PACK = 4
+BANK = 512
+HALF = 256
+
+
+def tile_attend_secondpick_twoq_mixed_kernel(
+    tc, query, query2, keys_words, keys_scales, notes_words, notes_scales, rowf,
+    mix_words, mix_scales, offs, offs2, offs3, offs4, offs5, out,
+):
+    nc = tc.nc
+    with ExitStack() as ctx:
+        lists = ctx.enter_context(tc.tile_pool(name="lists", bufs=1))
+        keep = ctx.enter_context(tc.tile_pool(name="keep", bufs=1))
+        psum = ctx.enter_context(tc.psum_pool(name="psum", bufs=1))
+        bank = [psum.tile([P, BANK], F32, name="bank_%d" % n) for n in range(8)]
+
+        def load_list(src, name):
+            held = lists.tile([P, src.shape[1]], U16, name=name)
+            nc.sync.dma_start(held[:], src)
+            return held
+
+        def scale_tile(width, name):
+            held = keep.tile([P, width], U8, name=name, align_bytes=64)
+            nc.vector.memset(held[:].bitcast(U32), 0)
+            return held
+
+        def load_scales(held, src):
+            for g in range(4):
+                nc.sync.dma_start(
+                    held[32 * g : 32 * g + 4, :].bitcast(I32),
+                    src[0, 4 * g : 4 * g + 4, :].bitcast(I32),
+                )
+
+        def load_query_half(src, h, name):
+            raw = keep.tile([P, PACK, HALF], F32, name=name)
+            nc.sync.dma_start(
+                raw[:], src.rearrange("(p j) q -> p j q", j=PACK)[:, :, h * HALF : (h + 1) * HALF]
+            )
+            return raw
+
+        def deal_half(dealt, raw, h):
+            half_m = HALF // PACK
+            dst = dealt[:].rearrange("p (t m j) -> p m t j", t=PACK, j=PACK)
+            nc.vector.tensor_copy(
+                dst[:, h * half_m : (h + 1) * half_m], raw[:].rearrange("p j (m t) -> p m t j", t=PACK)
+            )
+
+        def quantise(src, width, name):
+            codes = keep.tile([P, width], U32, name=name + "_codes", align_bytes=64)
+            scales = keep.tile([P, width], U8, name=name + "_scales", align_bytes=64)
+            nc.vector.quantize_mx(out=codes[:].bitcast(FP8X4), scales=scales[:], in_=src)
+            return codes, scales
+
+        notes_sc = scale_tile(U, "notes_sc")
+        keys_sc = scale_tile(T, "keys_sc")
+        mix_sc = scale_tile(E, "mix_sc")
+        f1 = [keep.tile([P, T], F32, name="f1_%d" % t) for t in range(4)]
+        for t in range(4):
+            (nc.gpsimd if t < 2 else nc.vector).memset(f1[t][:], 0.0)
+
+        q2_raw0 = load_query_half(query2, 0, "q2_raw0")
+        load_scales(notes_sc, notes_scales)
+        q2_raw1 = load_query_half(query2, 1, "q2_raw1")
+        notes_w = keep.tile([P, U], U32, name="notes_w", align_bytes=64)
+        nc.sync.dma_start(
+            notes_w[:].bitcast(I32), notes_words[0].rearrange("p n r -> p (n r)").bitcast(I32)
+        )
+        idx2 = load_list(offs2, "idx2")
+        q_raw0 = load_query_half(query, 0, "q_raw0")
+        q_raw1 = load_query_half(query, 1, "q_raw1")
+        keys_w = keep.tile([P, 2 * T], U8, name="keys_w", align_bytes=64)
+        nc.sync.dma_start(keys_w[:].bitcast(I32), keys_words[0].bitcast(I32))
+        load_scales(keys_sc, keys_scales)
+        idx = load_list(offs, "idx")
+        idx3 = load_list(offs3, "idx3")
+        idx4 = load_list(offs4, "idx4")
+        idx5 = load_list(offs5, "idx5")
+        rowf_sb = keep.tile([P, PACK], F32, name="rowf_sb")
+        nc.sync.dma_start(rowf_sb[:], rowf.rearrange("(p t) o -> p (t o)", t=PACK))
+        mix_w = keep.tile([P, E], U32, name="mix_w", align_bytes=64)
+        nc.sync.dma_start(
+            mix_w[:].bitcast(I32), mix_words[0].rearrange("p n r -> p (n r)").bitcast(I32)
+        )
+        load_scales(mix_sc, mix_scales)
+
+        q2_dealt = keep.tile([P, PACK * Q], BF16, name="q2_dealt", align_bytes=64)
+        deal_half(q2_dealt, q2_raw0, 0)
+        deal_half(q2_dealt, q2_raw1, 1)
+        q2_mx = [quantise(q2_dealt[:, u * 2 * Q : (u + 1) * 2 * Q], Q // 2, "q2_%d" % u) for u in range(2)]
+
+        banks = {}
+        b_at = {}
+
+        def scores(quantised, t, moving, moving_sc, tag, on_vector, pair):
+            table = keep.tile([P, 2 * BANK], F32, name="%s_%d" % (tag, t))
+            codes, scales = quantised[t // 2]
+            rows = slice(t % 2 * P, (t % 2 + 1) * P)
+            for n in range(2):
+                cols = slice(n * BANK, (n + 1) * BANK)
+                acc = bank[2 * pair + n]
+                nc.tensor.matmul_mx(
+                    out=acc[:], lhsT=codes[:, rows].bitcast(FP8X4), lhsT_scale=scales[:, rows],
+                    rhs=moving(n), rhs_scale=moving_sc[:, cols], start=True, stop=True,
+                )
+                banks[tag, t, n] = acc
+                if n in on_vector:
+                    nc.vector.tensor_copy(table[:, cols], acc[:])
+                else:
+                    nc.scalar.copy(table[:, cols], acc[:])
+            return table
+
+        def notes_moving(n):
+            return notes_w[:, n * BANK : (n + 1) * BANK].bitcast(FP8X4)
+
+        def keys_moving(n):
+            return keys_w[:, 2 * n * BANK : 2 * (n + 1) * BANK].bitcast(FP4X4)
+
+        a = {}
+        r = {}
+        w = {}
+        cc = {}
+
+        b = {}
+
+        def score_notes(t, on_vector, pair):
+            b[t] = scores(q2_mx, t, notes_moving, notes_sc, "b", on_vector, pair)
+
+        def note_at(t):
+            b_at[t] = keep.tile([P, I], F32, name="b_at_%d" % t)
+            nc.scalar.activation(b_at[t][:], b[t][:].indirect(idx2[:]), COPY)
+
+        def score_keys(t, on_vector, pair):
+            a[t] = scores(q_mx, t, keys_moving, keys_sc, "a", on_vector, pair)
+
+        def clock(src, name):
+            tick = keep.tile([P, 1], F32, name=name)
+            nc.gpsimd.tensor_copy(tick[:], src)
+
+        def lead(t):
+            r[t] = keep.tile([P, I], F32, name="r_%d" % t, tag="shared_%d" % t)
+            nc.vector.tensor_tensor(r[t][:], a[t][:].indirect(idx[:]), b_at[t][:], SUB)
+
+        def lead_split(t):
+            a_at = keep.tile([P, I], F32, name="a_at_%d" % t)
+            nc.scalar.activation(a_at[:], a[t][:].indirect(idx[:]), COPY)
+            r[t] = keep.tile([P, I], F32, name="r_%d" % t, tag="shared_%d" % t)
+            nc.vector.tensor_tensor(r[t][:], a_at[:], b_at[t][:], SUB)
+
+        def pick(t):
+            w[t] = keep.tile([P, J], F32, name="w_%d" % t)
+            nc.scalar.activation(w[t][:], r[t][:].indirect(idx3[:]), COPY, scale=2.0)
+
+        def place(t):
+            nc.vector.tensor_copy(f1[t % len(f1)][:].indirect(idx4[:]), w[t][:])
+
+        def add(t, eng):
+            cc[t] = keep.tile([P, T], F32, name="cc_%d" % t, tag="shared_%d" % (t ^ 1))
+            eng.tensor_tensor(cc[t][:], a[t][:], f1[t % len(f1)][:], ADD)
+
+        def add_from_banks(t):
+            cc[t] = keep.tile([P, T], F32, name="cc_%d" % t, tag="shared_%d" % (t ^ 1))
+            for n in range(2):
+                cols = slice(n * BANK, (n + 1) * BANK)
+                nc.vector.tensor_tensor(cc[t][:, cols], banks["a", t, n][:], f1[t % len(f1)][:, cols], ADD)
+
+        def result(t):
+            g = keep.tile([P, I], F32, name="g_%d" % t)
+            nc.scalar.activation(g[:], cc[t][:].indirect(idx5[:]), COPY)
+            for h in range(2):
+                nc.scalar.activation(
+                    gw32[h][:, t, :], g[:, h * HALF : (h + 1) * HALF], COPY, scale=rowf_sb[:, t : t + 1]
+                )
+
+        def last_result(t):
+            cut = HALF // 16
+            nc.vector.tensor_tensor(gw32[0][:, t, :], cc[t][:].indirect(idx5[:, :cut]), factor[:], MULT)
+            g = keep.tile([P, HALF], F32, name="g_last")
+            nc.scalar.activation(g[:], cc[t][:].indirect(idx5[:, cut:]), COPY)
+            nc.scalar.activation(gw32[1][:, t, :], g[:], COPY, scale=rowf_sb[:, t : t + 1])
+
+        def prepare_query():
+            q_dealt = keep.tile([P, PACK * Q], BF16, name="q_dealt", align_bytes=64)
+            deal_half(q_dealt, q_raw0, 0)
+            deal_half(q_dealt, q_raw1, 1)
+            return [quantise(q_dealt[:, u * 2 * Q : (u + 1) * 2 * Q], Q // 2, "q_%d" % u) for u in range(2)]
+
+        gw32 = [keep.tile([P, PACK, HALF], F32, name="gw32_%d" % h) for h in range(2)]
+        factor = keep.tile([P, HALF], F32, name="factor")
+        score_notes(0, (1,), 0)
+        q_mx = prepare_query()
+        score_notes(1, (), 1)
+        note_at(0)
+        note_at(1)
+        score_keys(0, (0, 1), 2)
+        score_keys(1, (), 3)
+        lead(0)
+        lead(1)
+        pick(0)
+        pick(1)
+        place(0)
+        place(1)
+        add(0, nc.vector)
+        add(1, nc.vector)
+        score_notes(2, (), 2)
+        note_at(2)
+        score_keys(2, (), 0)
+        score_notes(3, (), 3)
+        note_at(3)
+        score_keys(3, (), 1)
+        lead(2)
+        lead(3)
+        pick(2)
+        pick(3)
+        place(2)
+        place(3)
+        add(2, nc.vector)
+        add(3, nc.vector)
+        nc.scalar.copy(factor[:], rowf_sb[:, 3:4].to_broadcast([P, HALF]))
+        result(0)
+        result(1)
+        result(2)
+        last_result(3)
+
+        step = 4
+        for h in range(2):
+            slots = slice(h * HALF, (h + 1) * HALF)
+            gw = keep.tile([P, HALF * PACK], BF16, name="gw_%d" % h, align_bytes=64)
+            nc.vector.tensor_copy(
+                gw[:].rearrange("p (c i t) -> p c t i", i=step, t=PACK),
+                gw32[h][:].rearrange("p t (c i) -> p c t i", i=step),
+            )
+            gw_codes, gw_scales = quantise(gw[:], HALF, "gw_q%d" % h)
+            for m in range(E // P):
+                chans = slice(m * P, (m + 1) * P)
+                acc = bank[2 * h + m][:, :HALF]
+                nc.tensor.matmul_mx(
+                    out=acc, lhsT=mix_w[:, chans].bitcast(FP8X4), lhsT_scale=mix_sc[:, chans],
+                    rhs=gw_codes[:].bitcast(FP8X4), rhs_scale=gw_scales[:], start=True, stop=True,
+                )
+                y = keep.tile([P, HALF], F32, name="y_%d_%d" % (h, m))
+                if h == 1 and m == 1:
+                    nc.vector.tensor_copy(y[:], acc)
+                else:
+                    nc.scalar.copy(y[:], acc)
+                nc.sync.dma_start(out[chans, slots], y[:])

@@ -61,9 +61,9 @@ def tile_attend_secondpick_twoq_mixed_kernel(
 
         def deal_half(dealt, raw, h):
             half_m = HALF // PACK
-            dst = dealt[:].rearrange("p (t m j) -> p m t j", t=PACK, j=PACK)
+            dst = dealt[:].rearrange("p (t m j) -> p m j t", t=PACK, j=PACK)
             nc.vector.tensor_copy(
-                dst[:, h * half_m : (h + 1) * half_m], raw[:].rearrange("p j (m t) -> p m t j", t=PACK)
+                dst[:, h * half_m : (h + 1) * half_m], raw[:].rearrange("p j (m t) -> p m j t", t=PACK)
             )
 
         def quantise(src, width, name):
@@ -75,19 +75,19 @@ def tile_attend_secondpick_twoq_mixed_kernel(
         notes_sc = scale_tile(U, "notes_sc")
         keys_sc = scale_tile(T, "keys_sc")
         mix_sc = scale_tile(E, "mix_sc")
-        f1 = [keep.tile([P, T], F32, name="f1_%d" % t) for t in range(4)]
-        for t in range(4):
-            (nc.gpsimd if t < 2 else nc.vector).memset(f1[t][:], 0.0)
+        f1 = [keep.tile([P, T], F32, name="f1_%d" % t) for t in range(2)]
+        for t in range(2):
+            nc.vector.memset(f1[t][:], 0.0)
 
         q2_raw0 = load_query_half(query2, 0, "q2_raw0")
-        load_scales(notes_sc, notes_scales)
         q2_raw1 = load_query_half(query2, 1, "q2_raw1")
         notes_w = keep.tile([P, U], U32, name="notes_w", align_bytes=64)
         nc.sync.dma_start(
             notes_w[:].bitcast(I32), notes_words[0].rearrange("p n r -> p (n r)").bitcast(I32)
         )
-        idx2 = load_list(offs2, "idx2")
+        load_scales(notes_sc, notes_scales)
         q_raw0 = load_query_half(query, 0, "q_raw0")
+        idx2 = load_list(offs2, "idx2")
         q_raw1 = load_query_half(query, 1, "q_raw1")
         keys_w = keep.tile([P, 2 * T], U8, name="keys_w", align_bytes=64)
         nc.sync.dma_start(keys_w[:].bitcast(I32), keys_words[0].bitcast(I32))

@@ -53,7 +53,7 @@ def tile_attend_secondpick_twoq_mixed_kernel(
                 )
 
         def load_query_half(src, h, name):
-            raw = keep.tile([P, PACK, HALF], F32, name=name)
+            raw = keep.tile([P, PACK, HALF], F32, name=name, tag=name)
             nc.sync.dma_start(
                 raw[:], src.rearrange("(p j) q -> p j q", j=PACK)[:, :, h * HALF : (h + 1) * HALF]
             )
@@ -72,6 +72,8 @@ def tile_attend_secondpick_twoq_mixed_kernel(
             nc.vector.quantize_mx(out=codes[:].bitcast(FP8X4), scales=scales[:], in_=src)
             return codes, scales
 
+        rowf_sb = keep.tile([P, PACK], F32, name="rowf_sb")
+        nc.gpsimd.dma_start(rowf_sb[:], rowf.rearrange("(p t) o -> p (t o)", t=PACK))
         notes_sc = scale_tile(U, "notes_sc")
         keys_sc = scale_tile(T, "keys_sc")
         mix_sc = scale_tile(E, "mix_sc")
@@ -96,8 +98,6 @@ def tile_attend_secondpick_twoq_mixed_kernel(
         idx3 = load_list(offs3, "idx3")
         idx4 = load_list(offs4, "idx4")
         idx5 = load_list(offs5, "idx5")
-        rowf_sb = keep.tile([P, PACK], F32, name="rowf_sb")
-        nc.sync.dma_start(rowf_sb[:], rowf.rearrange("(p t) o -> p (t o)", t=PACK))
         mix_w = keep.tile([P, E], U32, name="mix_w", align_bytes=64)
         nc.sync.dma_start(
             mix_w[:].bitcast(I32), mix_words[0].rearrange("p n r -> p (n r)").bitcast(I32)
@@ -113,7 +113,8 @@ def tile_attend_secondpick_twoq_mixed_kernel(
         b_at = {}
 
         def scores(quantised, t, moving, moving_sc, tag, on_vector, pair):
-            table = keep.tile([P, 2 * BANK], F32, name="%s_%d" % (tag, t))
+            name = "%s_%d" % (tag, t)
+            table = keep.tile([P, 2 * BANK], F32, name=name, tag=name)
             codes, scales = quantised[t // 2]
             rows = slice(t % 2 * P, (t % 2 + 1) * P)
             for n in range(2):
@@ -147,7 +148,7 @@ def tile_attend_secondpick_twoq_mixed_kernel(
             b[t] = scores(q2_mx, t, notes_moving, notes_sc, "b", on_vector, pair)
 
         def note_at(t):
-            b_at[t] = keep.tile([P, I], F32, name="b_at_%d" % t)
+            b_at[t] = keep.tile([P, I], F32, name="b_at_%d" % t, tag="b_at_%d" % t)
             nc.scalar.activation(b_at[t][:], b[t][:].indirect(idx2[:]), COPY)
 
         def score_keys(t, on_vector, pair):
@@ -168,7 +169,7 @@ def tile_attend_secondpick_twoq_mixed_kernel(
             nc.vector.tensor_tensor(r[t][:], a_at[:], b_at[t][:], SUB)
 
         def pick(t):
-            w[t] = keep.tile([P, J], F32, name="w_%d" % t)
+            w[t] = keep.tile([P, J], F32, name="w_%d" % t, tag="b_3" if t == 2 else "w_%d" % t)
             nc.scalar.activation(w[t][:], r[t][:].indirect(idx3[:]), COPY, scale=2.0)
 
         def place(t):
@@ -192,10 +193,13 @@ def tile_attend_secondpick_twoq_mixed_kernel(
                     gw32[h][:, t, :], g[:, h * HALF : (h + 1) * HALF], COPY, scale=rowf_sb[:, t : t + 1]
                 )
 
-        def last_result(t):
-            cut = HALF // 16
-            nc.vector.tensor_tensor(gw32[0][:, t, :], cc[t][:].indirect(idx5[:, :cut]), factor[:], MULT)
-            g = keep.tile([P, HALF], F32, name="g_last")
+        cut = HALF // 16
+
+        def first_half(t):
+            nc.vector.tensor_tensor(gw32[0][:, t, :], cc[t][:].indirect(idx5[:, :cut]), factor[t][:], MULT)
+
+        def second_half(t):
+            g = keep.tile([P, HALF], F32, name="g_late_%d" % t)
             nc.scalar.activation(g[:], cc[t][:].indirect(idx5[:, cut:]), COPY)
             nc.scalar.activation(gw32[1][:, t, :], g[:], COPY, scale=rowf_sb[:, t : t + 1])
 
@@ -206,7 +210,10 @@ def tile_attend_secondpick_twoq_mixed_kernel(
             return [quantise(q_dealt[:, u * 2 * Q : (u + 1) * 2 * Q], Q // 2, "q_%d" % u) for u in range(2)]
 
         gw32 = [keep.tile([P, PACK, HALF], F32, name="gw32_%d" % h) for h in range(2)]
-        factor = keep.tile([P, HALF], F32, name="factor")
+        factor = {}
+        for t in (2, 3):
+            factor[t] = keep.tile([P, HALF], F32, name="factor_%d" % t)
+            nc.scalar.copy(factor[t][:], rowf_sb[:, t : t + 1].to_broadcast([P, HALF]))
         score_notes(0, (1,), 0)
         q_mx = prepare_query()
         score_notes(1, (), 1)
@@ -220,27 +227,28 @@ def tile_attend_secondpick_twoq_mixed_kernel(
         pick(1)
         place(0)
         place(1)
-        add(0, nc.vector)
-        add(1, nc.vector)
+        add(0, nc.gpsimd)
+        add_from_banks(1)
         score_notes(2, (), 2)
         note_at(2)
         score_keys(2, (), 0)
-        score_notes(3, (), 3)
+        score_notes(3, (), 2)
         note_at(3)
-        score_keys(3, (), 1)
+        score_keys(3, (0,), 1)
         lead(2)
         lead(3)
         pick(2)
         pick(3)
         place(2)
         place(3)
-        add(2, nc.vector)
-        add(3, nc.vector)
-        nc.scalar.copy(factor[:], rowf_sb[:, 3:4].to_broadcast([P, HALF]))
+        add(2, nc.gpsimd)
+        add_from_banks(3)
         result(0)
         result(1)
-        result(2)
-        last_result(3)
+        first_half(2)
+        second_half(2)
+        first_half(3)
+        second_half(3)
 
         step = 4
         for h in range(2):
@@ -253,7 +261,7 @@ def tile_attend_secondpick_twoq_mixed_kernel(
             gw_codes, gw_scales = quantise(gw[:], HALF, "gw_q%d" % h)
             for m in range(E // P):
                 chans = slice(m * P, (m + 1) * P)
-                acc = bank[2 * h + m][:, :HALF]
+                acc = bank[4 * h + m][:, :HALF]
                 nc.tensor.matmul_mx(
                     out=acc, lhsT=mix_w[:, chans].bitcast(FP8X4), lhsT_scale=mix_sc[:, chans],
                     rhs=gw_codes[:].bitcast(FP8X4), rhs_scale=gw_scales[:], start=True, stop=True,

@@ -20,8 +20,14 @@ COPY = mybir.ActivationFunctionType.Copy
 
 P = 128
 PACK = 4
+QUADRANT = 32
 BANK = 512
-HALF = 256
+BANKS = 8
+LIST_ROWS = 16
+Q_HALF = Q // 2
+I_HALF = I // 2
+F1_TILES = 3
+LINE = 4
 
 
 def tile_attend_secondpick_twoq_mixed_kernel(
@@ -33,64 +39,55 @@ def tile_attend_secondpick_twoq_mixed_kernel(
         lists = ctx.enter_context(tc.tile_pool(name="lists", bufs=1))
         keep = ctx.enter_context(tc.tile_pool(name="keep", bufs=1))
         psum = ctx.enter_context(tc.psum_pool(name="psum", bufs=1))
-        bank = [psum.tile([P, BANK], F32, name="bank_%d" % n) for n in range(8)]
+        bank = [psum.tile([P, BANK], F32, name="bank_%d" % n) for n in range(BANKS)]
+
 
         def load_list(src, name):
             held = lists.tile([P, src.shape[1]], U16, name=name)
             nc.sync.dma_start(held[:], src)
             return held
 
-        def scale_tile(width, name):
+        def zeroed_scales(width, name):
             held = keep.tile([P, width], U8, name=name, align_bytes=64)
             nc.vector.memset(held[:].bitcast(U32), 0)
             return held
 
         def load_scales(held, src):
-            for g in range(4):
+            for n in range(P // QUADRANT):
                 nc.sync.dma_start(
-                    held[32 * g : 32 * g + 4, :].bitcast(I32),
-                    src[0, 4 * g : 4 * g + 4, :].bitcast(I32),
+                    held[QUADRANT * n : QUADRANT * n + 4, :].bitcast(I32),
+                    src[0, 4 * n : 4 * n + 4, :].bitcast(I32),
                 )
 
-        def load_query_half(src, h, name):
-            raw = keep.tile([P, PACK, HALF], F32, name=name, tag=name)
+        def load_e4m3_words(src, name):
+            held = keep.tile([P, src.shape[2]], U32, name=name, align_bytes=64)
             nc.sync.dma_start(
-                raw[:], src.rearrange("(p j) q -> p j q", j=PACK)[:, :, h * HALF : (h + 1) * HALF]
+                held[:].bitcast(I32), src[0].rearrange("p n j -> p (n j)").bitcast(I32)
             )
+            return held
+
+        def load_query_half(src, h, name):
+            raw = keep.tile([P, PACK, Q_HALF], F32, name=name)
+            by_word = src.rearrange("(p j) q -> p j q", j=PACK)
+            nc.sync.dma_start(raw[:], by_word[:, :, h * Q_HALF : (h + 1) * Q_HALF])
             return raw
-
-        def deal_half(dealt, raw, h):
-            half_m = HALF // PACK
-            dst = dealt[:].rearrange("p (t m j) -> p m j t", t=PACK, j=PACK)
-            nc.vector.tensor_copy(
-                dst[:, h * half_m : (h + 1) * half_m], raw[:].rearrange("p j (m t) -> p m j t", t=PACK)
-            )
-
-        def quantise(src, width, name):
-            codes = keep.tile([P, width], U32, name=name + "_codes", align_bytes=64)
-            scales = keep.tile([P, width], U8, name=name + "_scales", align_bytes=64)
-            nc.vector.quantize_mx(out=codes[:].bitcast(FP8X4), scales=scales[:], in_=src)
-            return codes, scales
 
         rowf_sb = keep.tile([P, PACK], F32, name="rowf_sb")
         nc.gpsimd.dma_start(rowf_sb[:], rowf.rearrange("(p t) o -> p (t o)", t=PACK))
-        notes_sc = scale_tile(U, "notes_sc")
-        keys_sc = scale_tile(T, "keys_sc")
-        mix_sc = scale_tile(E, "mix_sc")
-        f1 = [keep.tile([P, T], F32, name="f1_%d" % t) for t in range(2)]
-        for t in range(2):
-            nc.vector.memset(f1[t][:], 0.0)
 
-        q2_raw0 = load_query_half(query2, 0, "q2_raw0")
-        q2_raw1 = load_query_half(query2, 1, "q2_raw1")
-        notes_w = keep.tile([P, U], U32, name="notes_w", align_bytes=64)
-        nc.sync.dma_start(
-            notes_w[:].bitcast(I32), notes_words[0].rearrange("p n r -> p (n r)").bitcast(I32)
-        )
+        notes_sc = zeroed_scales(U, "notes_sc")
+        keys_sc = zeroed_scales(T, "keys_sc")
+        mix_sc = zeroed_scales(E, "mix_sc")
+        f1 = [keep.tile([P, T], F32, name="f1_%d" % n) for n in range(F1_TILES)]
+        for n in range(F1_TILES):
+            nc.vector.memset(f1[n][:], 0.0)
+
+        q2_raw = [load_query_half(query2, h, "q2_raw_%d" % h) for h in range(2)]
+        notes_w = load_e4m3_words(notes_words, "notes_w")
         load_scales(notes_sc, notes_scales)
-        q_raw0 = load_query_half(query, 0, "q_raw0")
+        q_raw = [load_query_half(query, 0, "q_raw_0")]
         idx2 = load_list(offs2, "idx2")
-        q_raw1 = load_query_half(query, 1, "q_raw1")
+        q_raw.append(load_query_half(query, 1, "q_raw_1"))
         keys_w = keep.tile([P, 2 * T], U8, name="keys_w", align_bytes=64)
         nc.sync.dma_start(keys_w[:].bitcast(I32), keys_words[0].bitcast(I32))
         load_scales(keys_sc, keys_scales)
@@ -98,177 +95,156 @@ def tile_attend_secondpick_twoq_mixed_kernel(
         idx3 = load_list(offs3, "idx3")
         idx4 = load_list(offs4, "idx4")
         idx5 = load_list(offs5, "idx5")
-        mix_w = keep.tile([P, E], U32, name="mix_w", align_bytes=64)
-        nc.sync.dma_start(
-            mix_w[:].bitcast(I32), mix_words[0].rearrange("p n r -> p (n r)").bitcast(I32)
-        )
+        mix_w = load_e4m3_words(mix_words, "mix_w")
         load_scales(mix_sc, mix_scales)
 
-        q2_dealt = keep.tile([P, PACK * Q], BF16, name="q2_dealt", align_bytes=64)
-        deal_half(q2_dealt, q2_raw0, 0)
-        deal_half(q2_dealt, q2_raw1, 1)
-        q2_mx = [quantise(q2_dealt[:, u * 2 * Q : (u + 1) * 2 * Q], Q // 2, "q2_%d" % u) for u in range(2)]
 
-        banks = {}
-        b_at = {}
+        def quantise(src, width, name):
+            codes = keep.tile([P, width], U32, name=name + "_codes", align_bytes=64)
+            scales = keep.tile([P, width], U8, name=name + "_scales", align_bytes=64)
+            nc.vector.quantize_mx(out=codes[:].bitcast(FP8X4), scales=scales[:], in_=src)
+            return codes, scales
 
-        def scores(quantised, t, moving, moving_sc, tag, on_vector, pair):
-            name = "%s_%d" % (tag, t)
-            table = keep.tile([P, 2 * BANK], F32, name=name, tag=name)
-            codes, scales = quantised[t // 2]
-            rows = slice(t % 2 * P, (t % 2 + 1) * P)
+        def quantise_queries(raw, name):
+            dealt = keep.tile([P, PACK * Q], BF16, name=name + "_dealt", align_bytes=64)
+            dealt_view = dealt[:].rearrange("p (t m j) -> p m j t", t=PACK, j=PACK)
+            m_half = Q_HALF // PACK
+            for h in range(2):
+                nc.vector.tensor_copy(
+                    dealt_view[:, h * m_half : (h + 1) * m_half],
+                    raw[h][:].rearrange("p j (m t) -> p m j t", t=PACK),
+                )
+            width = P * PACK
+            return [
+                quantise(dealt[:, t * width : (t + 1) * width], P, "%s_%d" % (name, t))
+                for t in range(PACK)
+            ]
+
+        def scores(name, stationary, moving, moving_sc, pair, copies):
+            table = keep.tile([P, 2 * BANK], F32, name=name)
+            codes, scales = stationary
             for n in range(2):
                 cols = slice(n * BANK, (n + 1) * BANK)
                 acc = bank[2 * pair + n]
                 nc.tensor.matmul_mx(
-                    out=acc[:], lhsT=codes[:, rows].bitcast(FP8X4), lhsT_scale=scales[:, rows],
-                    rhs=moving(n), rhs_scale=moving_sc[:, cols], start=True, stop=True,
+                    out=acc[:], lhsT=codes[:].bitcast(FP8X4), lhsT_scale=scales[:],
+                    rhs=moving[n], rhs_scale=moving_sc[:, cols], start=True, stop=True,
                 )
-                banks[tag, t, n] = acc
-                if n in on_vector:
-                    nc.vector.tensor_copy(table[:, cols], acc[:])
-                else:
-                    nc.scalar.copy(table[:, cols], acc[:])
+                copies[n](table[:, cols], acc[:])
             return table
 
-        def notes_moving(n):
-            return notes_w[:, n * BANK : (n + 1) * BANK].bitcast(FP8X4)
+        notes_moving = [notes_w[:, n * BANK : (n + 1) * BANK].bitcast(FP8X4) for n in range(2)]
+        keys_moving = [keys_w[:, 2 * n * BANK : 2 * (n + 1) * BANK].bitcast(FP4X4) for n in range(2)]
+        by_scalar, by_vector = nc.scalar.copy, nc.vector.tensor_copy
+        a, b, b_at, r, w, cc = {}, {}, {}, {}, {}, {}
 
-        def keys_moving(n):
-            return keys_w[:, 2 * n * BANK : 2 * (n + 1) * BANK].bitcast(FP4X4)
+        def score_notes(t, copies):
+            b[t] = scores("b_%d" % t, q2_mx[t], notes_moving, notes_sc, t, copies)
 
-        a = {}
-        r = {}
-        w = {}
-        cc = {}
+        def score_keys(t, copies):
+            a[t] = scores("a_%d" % t, q_mx[t], keys_moving, keys_sc, t ^ 2, copies)
 
-        b = {}
-
-        def score_notes(t, on_vector, pair):
-            b[t] = scores(q2_mx, t, notes_moving, notes_sc, "b", on_vector, pair)
-
-        def note_at(t):
-            b_at[t] = keep.tile([P, I], F32, name="b_at_%d" % t, tag="b_at_%d" % t)
+        def look_up_notes(t):
+            b_at[t] = keep.tile([P, I], F32, name="b_at_%d" % t)
             nc.scalar.activation(b_at[t][:], b[t][:].indirect(idx2[:]), COPY)
 
-        def score_keys(t, on_vector, pair):
-            a[t] = scores(q_mx, t, keys_moving, keys_sc, "a", on_vector, pair)
-
-        def clock(src, name):
-            tick = keep.tile([P, 1], F32, name=name)
-            nc.gpsimd.tensor_copy(tick[:], src)
-
         def lead(t):
-            r[t] = keep.tile([P, I], F32, name="r_%d" % t, tag="shared_%d" % t)
+            r[t] = keep.tile([P, I], F32, name="r_%d" % t)
             nc.vector.tensor_tensor(r[t][:], a[t][:].indirect(idx[:]), b_at[t][:], SUB)
 
-        def lead_split(t):
-            a_at = keep.tile([P, I], F32, name="a_at_%d" % t)
-            nc.scalar.activation(a_at[:], a[t][:].indirect(idx[:]), COPY)
-            r[t] = keep.tile([P, I], F32, name="r_%d" % t, tag="shared_%d" % t)
-            nc.vector.tensor_tensor(r[t][:], a_at[:], b_at[t][:], SUB)
-
         def pick(t):
-            w[t] = keep.tile([P, J], F32, name="w_%d" % t, tag="b_3" if t == 2 else "w_%d" % t)
+            w[t] = keep.tile([P, J], F32, name="w_%d" % t)
             nc.scalar.activation(w[t][:], r[t][:].indirect(idx3[:]), COPY, scale=2.0)
 
         def place(t):
-            nc.vector.tensor_copy(f1[t % len(f1)][:].indirect(idx4[:]), w[t][:])
+            nc.vector.tensor_copy(f1[t % F1_TILES][:].indirect(idx4[:]), w[t][:])
 
-        def add(t, eng):
-            cc[t] = keep.tile([P, T], F32, name="cc_%d" % t, tag="shared_%d" % (t ^ 1))
-            eng.tensor_tensor(cc[t][:], a[t][:], f1[t % len(f1)][:], ADD)
+        def add_on_gpsimd(t, tag):
+            cc[t] = keep.tile([P, T], F32, name="cc_%d" % t, tag=tag)
+            nc.gpsimd.tensor_tensor(cc[t][:], a[t][:], f1[t % F1_TILES][:], ADD)
 
         def add_from_banks(t):
-            cc[t] = keep.tile([P, T], F32, name="cc_%d" % t, tag="shared_%d" % (t ^ 1))
+            cc[t] = keep.tile([P, T], F32, name="cc_%d" % t)
             for n in range(2):
                 cols = slice(n * BANK, (n + 1) * BANK)
-                nc.vector.tensor_tensor(cc[t][:, cols], banks["a", t, n][:], f1[t % len(f1)][:, cols], ADD)
-
-        def result(t):
-            g = keep.tile([P, I], F32, name="g_%d" % t)
-            nc.scalar.activation(g[:], cc[t][:].indirect(idx5[:]), COPY)
-            for h in range(2):
-                nc.scalar.activation(
-                    gw32[h][:, t, :], g[:, h * HALF : (h + 1) * HALF], COPY, scale=rowf_sb[:, t : t + 1]
+                nc.vector.tensor_tensor(
+                    cc[t][:, cols], bank[2 * (t ^ 2) + n][:], f1[t % F1_TILES][:, cols], ADD
                 )
 
-        cut = HALF // 16
+        gw = [keep.tile([P, PACK, I_HALF], F32, name="gw_%d" % h) for h in range(2)]
+        list_half = I_HALF // LIST_ROWS
+        idx5_half = [idx5[:, :list_half], idx5[:, list_half:]]
 
-        def first_half(t):
-            nc.vector.tensor_tensor(gw32[0][:, t, :], cc[t][:].indirect(idx5[:, :cut]), factor[t][:], MULT)
+        def results_on_scalar(t, halves, tag):
+            g = keep.tile([P, len(halves), I_HALF], F32, name="g_%d" % t, tag=tag)
+            for n, h in enumerate(halves):
+                nc.scalar.activation(g[:, n, :], cc[t][:].indirect(idx5_half[h]), COPY)
+            for n, h in enumerate(halves):
+                nc.scalar.activation(gw[h][:, t, :], g[:, n, :], COPY, scale=rowf_sb[:, t : t + 1])
 
-        def second_half(t):
-            g = keep.tile([P, HALF], F32, name="g_late_%d" % t)
-            nc.scalar.activation(g[:], cc[t][:].indirect(idx5[:, cut:]), COPY)
-            nc.scalar.activation(gw32[1][:, t, :], g[:], COPY, scale=rowf_sb[:, t : t + 1])
+        def result_on_vector(t, h):
+            nc.vector.tensor_tensor(
+                gw[h][:, t, :], cc[t][:].indirect(idx5_half[h]), factor[t][:], MULT
+            )
 
-        def prepare_query():
-            q_dealt = keep.tile([P, PACK * Q], BF16, name="q_dealt", align_bytes=64)
-            deal_half(q_dealt, q_raw0, 0)
-            deal_half(q_dealt, q_raw1, 1)
-            return [quantise(q_dealt[:, u * 2 * Q : (u + 1) * 2 * Q], Q // 2, "q_%d" % u) for u in range(2)]
 
-        gw32 = [keep.tile([P, PACK, HALF], F32, name="gw32_%d" % h) for h in range(2)]
+        q2_mx = quantise_queries(q2_raw, "q2")
         factor = {}
         for t in (2, 3):
-            factor[t] = keep.tile([P, HALF], F32, name="factor_%d" % t)
-            nc.scalar.copy(factor[t][:], rowf_sb[:, t : t + 1].to_broadcast([P, HALF]))
-        score_notes(0, (1,), 0)
-        q_mx = prepare_query()
-        score_notes(1, (), 1)
-        note_at(0)
-        note_at(1)
-        score_keys(0, (0, 1), 2)
-        score_keys(1, (), 3)
-        lead(0)
-        lead(1)
-        pick(0)
-        pick(1)
-        place(0)
-        place(1)
-        add(0, nc.gpsimd)
-        add_from_banks(1)
-        score_notes(2, (), 2)
-        note_at(2)
-        score_keys(2, (), 0)
-        score_notes(3, (), 2)
-        note_at(3)
-        score_keys(3, (0,), 1)
-        lead(2)
-        lead(3)
-        pick(2)
-        pick(3)
-        place(2)
-        place(3)
-        add(2, nc.gpsimd)
-        add_from_banks(3)
-        result(0)
-        result(1)
-        first_half(2)
-        second_half(2)
-        first_half(3)
-        second_half(3)
+            factor[t] = keep.tile([P, I_HALF], F32, name="factor_%d" % t)
+            nc.scalar.copy(factor[t][:], rowf_sb[:, t : t + 1].to_broadcast([P, I_HALF]))
 
-        step = 4
+        score_notes(0, (by_scalar, by_vector))
+        q_mx = quantise_queries(q_raw, "q")
+        score_notes(1, (by_scalar, by_scalar))
+        for t in (0, 1):
+            look_up_notes(t)
+        score_keys(0, (by_vector, by_vector))
+        score_keys(1, (by_scalar, by_scalar))
+        for step in (lead, pick, place):
+            for t in (0, 1):
+                step(t)
+        add_on_gpsimd(0, "cc_0")
+
+
+        for t in (2, 3):
+            score_notes(t, (by_scalar, by_scalar))
+        look_up_notes(2)
+        score_keys(2, (by_scalar, by_scalar))
+        look_up_notes(3)
+        score_keys(3, (by_vector, by_vector))
+        for step in (lead, pick, place):
+            for t in (2, 3):
+                step(t)
+        add_on_gpsimd(1, "b_at_3")
+        add_on_gpsimd(2, "cc_2")
+        add_from_banks(3)
+
+
+        results_on_scalar(0, (0, 1), "r_3")
+        results_on_scalar(1, (0, 1), "g_1")
+        result_on_vector(2, 0)
+        results_on_scalar(2, (1,), "g_2")
+        result_on_vector(3, 0)
+        results_on_scalar(3, (1,), "g_1")
+
+
         for h in range(2):
-            slots = slice(h * HALF, (h + 1) * HALF)
-            gw = keep.tile([P, HALF * PACK], BF16, name="gw_%d" % h, align_bytes=64)
+            slots = slice(h * I_HALF, (h + 1) * I_HALF)
+            gw_bf16 = keep.tile([P, I_HALF * PACK], BF16, name="gw_bf16_%d" % h, align_bytes=64)
             nc.vector.tensor_copy(
-                gw[:].rearrange("p (c i t) -> p c t i", i=step, t=PACK),
-                gw32[h][:].rearrange("p t (c i) -> p c t i", i=step),
+                gw_bf16[:].rearrange("p (c i t) -> p c t i", i=LINE, t=PACK),
+                gw[h][:].rearrange("p t (c i) -> p c t i", i=LINE),
             )
-            gw_codes, gw_scales = quantise(gw[:], HALF, "gw_q%d" % h)
+            gw_codes, gw_scales = quantise(gw_bf16[:], I_HALF, "gw_mx_%d" % h)
             for m in range(E // P):
                 chans = slice(m * P, (m + 1) * P)
-                acc = bank[4 * h + m][:, :HALF]
+                acc = bank[4 * h + m][:, :I_HALF]
                 nc.tensor.matmul_mx(
                     out=acc, lhsT=mix_w[:, chans].bitcast(FP8X4), lhsT_scale=mix_sc[:, chans],
                     rhs=gw_codes[:].bitcast(FP8X4), rhs_scale=gw_scales[:], start=True, stop=True,
                 )
-                y = keep.tile([P, HALF], F32, name="y_%d_%d" % (h, m))
-                if h == 1 and m == 1:
-                    nc.vector.tensor_copy(y[:], acc)
-                else:
-                    nc.scalar.copy(y[:], acc)
+                y = keep.tile([P, I_HALF], F32, name="y_%d_%d" % (h, m))
+                copy_out = by_vector if (h, m) == (1, 1) else by_scalar
+                copy_out(y[:], acc)
                 nc.sync.dma_start(out[chans, slots], y[:])

@@ -66,10 +66,10 @@ def tile_attend_secondpick_twoq_mixed_kernel(
             )
             return held
 
-        def load_query_half(src, h, name):
-            raw = keep.tile([P, PACK, Q_HALF], F32, name=name)
+        def load_queries(src, first, width, name):
+            raw = keep.tile([P, PACK, width], F32, name=name)
             by_word = src.rearrange("(p j) q -> p j q", j=PACK)
-            nc.sync.dma_start(raw[:], by_word[:, :, h * Q_HALF : (h + 1) * Q_HALF])
+            nc.sync.dma_start(raw[:], by_word[:, :, first : first + width])
             return raw
 
         rowf_sb = keep.tile([P, PACK], F32, name="rowf_sb")
@@ -82,12 +82,11 @@ def tile_attend_secondpick_twoq_mixed_kernel(
         for n in range(F1_TILES):
             nc.vector.memset(f1[n][:], 0.0)
 
-        q2_raw = [load_query_half(query2, h, "q2_raw_%d" % h) for h in range(2)]
+        q2_raw = [load_queries(query2, h * Q_HALF, Q_HALF, "q2_raw_%d" % h) for h in range(2)]
         notes_w = load_e4m3_words(notes_words, "notes_w")
         load_scales(notes_sc, notes_scales)
-        q_raw = [load_query_half(query, 0, "q_raw_0")]
+        q_raw = load_queries(query, 0, Q, "q_raw")
         idx2 = load_list(offs2, "idx2")
-        q_raw.append(load_query_half(query, 1, "q_raw_1"))
         keys_w = keep.tile([P, 2 * T], U8, name="keys_w", align_bytes=64)
         nc.sync.dma_start(keys_w[:].bitcast(I32), keys_words[0].bitcast(I32))
         load_scales(keys_sc, keys_scales)
@@ -105,20 +104,29 @@ def tile_attend_secondpick_twoq_mixed_kernel(
             nc.vector.quantize_mx(out=codes[:].bitcast(FP8X4), scales=scales[:], in_=src)
             return codes, scales
 
-        def quantise_queries(raw, name):
-            dealt = keep.tile([P, PACK * Q], BF16, name=name + "_dealt", align_bytes=64)
-            dealt_view = dealt[:].rearrange("p (t m j) -> p m j t", t=PACK, j=PACK)
+        def by_rows(dealt):
+            return dealt[:].rearrange("p t (m j) -> p m j t", j=PACK)
+
+        def by_rows_raw(raw):
+            return raw[:].rearrange("p j (m t) -> p m j t", t=PACK)
+
+        def quantise_query2():
+            dealt = keep.tile([P, PACK, P * PACK], BF16, name="q2_dealt", align_bytes=64)
             m_half = Q_HALF // PACK
             for h in range(2):
                 nc.vector.tensor_copy(
-                    dealt_view[:, h * m_half : (h + 1) * m_half],
-                    raw[h][:].rearrange("p j (m t) -> p m j t", t=PACK),
+                    by_rows(dealt)[:, h * m_half : (h + 1) * m_half], by_rows_raw(q2_raw[h])
                 )
-            width = P * PACK
-            return [
-                quantise(dealt[:, t * width : (t + 1) * width], P, "%s_%d" % (name, t))
-                for t in range(PACK)
-            ]
+            for t in range(PACK):
+                q2_mx[t] = quantise(dealt[:, t, :], P, "q2_%d" % t)
+
+        def quantise_query_pair(first):
+            dealt = keep.tile([P, 2, P * PACK], BF16, name="q_dealt_%d" % first, align_bytes=64)
+            nc.vector.tensor_copy(by_rows(dealt), by_rows_raw(q_raw)[:, :, :, first : first + 2])
+            for n in range(2):
+                q_mx[first + n] = quantise(dealt[:, n, :], P, "q_%d" % (first + n))
+
+        q_mx, q2_mx = {}, {}
 
         def scores(name, stationary, moving, moving_sc, pair, copies):
             table = keep.tile([P, 2 * BANK], F32, name=name)
@@ -188,14 +196,14 @@ def tile_attend_secondpick_twoq_mixed_kernel(
             )
 
 
-        q2_mx = quantise_queries(q2_raw, "q2")
+        quantise_query2()
         factor = {}
         for t in (2, 3):
             factor[t] = keep.tile([P, I_HALF], F32, name="factor_%d" % t)
             nc.scalar.copy(factor[t][:], rowf_sb[:, t : t + 1].to_broadcast([P, I_HALF]))
 
         score_notes(0, (by_scalar, by_vector))
-        q_mx = quantise_queries(q_raw, "q")
+        quantise_query_pair(0)
         score_notes(1, (by_scalar, by_scalar))
         for t in (0, 1):
             look_up_notes(t)
@@ -207,6 +215,7 @@ def tile_attend_secondpick_twoq_mixed_kernel(
         add_on_gpsimd(0, "cc_0")
 
 
+        quantise_query_pair(2)
         for t in (2, 3):
             score_notes(t, (by_scalar, by_scalar))
         look_up_notes(2)

from contextlib import ExitStack

import concourse.mybir as mybir

D, T, U, I, J, Q, E = 512, 1024, 1024, 512, 256, 512, 256
FLOPS = 2 * D * Q * T + 2 * D * Q * U + 2 * Q * E * I

F32 = mybir.dt.float32
BF16 = mybir.dt.bfloat16
I32 = mybir.dt.int32
U32 = mybir.dt.uint32
U16 = mybir.dt.uint16
U8 = mybir.dt.uint8
FP8X4 = mybir.dt.float8_e4m3fn_x4
FP4X4 = mybir.dt.float4_e2m1fn_x4
ADD = mybir.AluOpType.add
SUB = mybir.AluOpType.subtract
MULT = mybir.AluOpType.mult
COPY = mybir.ActivationFunctionType.Copy

P = 128
PACK = 4
QUADRANT = 32
BANK = 512
BANKS = 8
LIST_ROWS = 16
Q_HALF = Q // 2
I_HALF = I // 2
F1_TILES = 3
LINE = 4


def tile_attend_secondpick_twoq_mixed_kernel(
    tc, query, query2, keys_words, keys_scales, notes_words, notes_scales, rowf,
    mix_words, mix_scales, offs, offs2, offs3, offs4, offs5, out,
):
    nc = tc.nc
    with ExitStack() as ctx:
        lists = ctx.enter_context(tc.tile_pool(name="lists", bufs=1))
        keep = ctx.enter_context(tc.tile_pool(name="keep", bufs=1))
        psum = ctx.enter_context(tc.psum_pool(name="psum", bufs=1))
        bank = [psum.tile([P, BANK], F32, name="bank_%d" % n) for n in range(BANKS)]


        def load_list(src, name):
            held = lists.tile([P, src.shape[1]], U16, name=name)
            nc.sync.dma_start(held[:], src)
            return held

        def zeroed_scales(width, name):
            held = keep.tile([P, width], U8, name=name, align_bytes=64)
            nc.vector.memset(held[:].bitcast(U32), 0)
            return held

        def load_scales(held, src):
            for n in range(P // QUADRANT):
                nc.sync.dma_start(
                    held[QUADRANT * n : QUADRANT * n + 4, :].bitcast(I32),
                    src[0, 4 * n : 4 * n + 4, :].bitcast(I32),
                )

        def load_e4m3_words(src, name):
            held = keep.tile([P, src.shape[2]], U32, name=name, align_bytes=64)
            nc.sync.dma_start(
                held[:].bitcast(I32), src[0].rearrange("p n j -> p (n j)").bitcast(I32)
            )
            return held

        def load_queries(src, first, width, name):
            raw = keep.tile([P, PACK, width], F32, name=name)
            by_word = src.rearrange("(p j) q -> p j q", j=PACK)
            nc.sync.dma_start(raw[:], by_word[:, :, first : first + width])
            return raw

        rowf_sb = keep.tile([P, PACK], F32, name="rowf_sb")
        nc.gpsimd.dma_start(rowf_sb[:], rowf.rearrange("(p t) o -> p (t o)", t=PACK))

        notes_sc = zeroed_scales(U, "notes_sc")
        keys_sc = zeroed_scales(T, "keys_sc")
        mix_sc = zeroed_scales(E, "mix_sc")
        f1 = [keep.tile([P, T], F32, name="f1_%d" % n) for n in range(F1_TILES)]
        for n in range(F1_TILES):
            nc.vector.memset(f1[n][:], 0.0)

        q2_raw = [load_queries(query2, h * Q_HALF, Q_HALF, "q2_raw_%d" % h) for h in range(2)]
        notes_w = load_e4m3_words(notes_words, "notes_w")
        load_scales(notes_sc, notes_scales)
        q_raw = load_queries(query, 0, Q, "q_raw")
        idx2 = load_list(offs2, "idx2")
        keys_w = keep.tile([P, 2 * T], U8, name="keys_w", align_bytes=64)
        nc.sync.dma_start(keys_w[:].bitcast(I32), keys_words[0].bitcast(I32))
        load_scales(keys_sc, keys_scales)
        idx = load_list(offs, "idx")
        idx3 = load_list(offs3, "idx3")
        idx4 = load_list(offs4, "idx4")
        idx5 = load_list(offs5, "idx5")
        mix_w = load_e4m3_words(mix_words, "mix_w")
        load_scales(mix_sc, mix_scales)


        def quantise(src, width, name):
            codes = keep.tile([P, width], U32, name=name + "_codes", align_bytes=64)
            scales = keep.tile([P, width], U8, name=name + "_scales", align_bytes=64)
            nc.vector.quantize_mx(out=codes[:].bitcast(FP8X4), scales=scales[:], in_=src)
            return codes, scales

        def by_rows(dealt):
            return dealt[:].rearrange("p t (m j) -> p m j t", j=PACK)

        def by_rows_raw(raw):
            return raw[:].rearrange("p j (m t) -> p m j t", t=PACK)

        def quantise_query2():
            dealt = keep.tile([P, PACK, P * PACK], BF16, name="q2_dealt", align_bytes=64)
            m_half = Q_HALF // PACK
            for h in range(2):
                nc.vector.tensor_copy(
                    by_rows(dealt)[:, h * m_half : (h + 1) * m_half], by_rows_raw(q2_raw[h])
                )
            for t in range(PACK):
                q2_mx[t] = quantise(dealt[:, t, :], P, "q2_%d" % t)

        def quantise_query_pair(first):
            dealt = keep.tile([P, 2, P * PACK], BF16, name="q_dealt_%d" % first, align_bytes=64)
            nc.vector.tensor_copy(by_rows(dealt), by_rows_raw(q_raw)[:, :, :, first : first + 2])
            for n in range(2):
                q_mx[first + n] = quantise(dealt[:, n, :], P, "q_%d" % (first + n))

        q_mx, q2_mx = {}, {}

        def scores(name, stationary, moving, moving_sc, pair, copies):
            table = keep.tile([P, 2 * BANK], F32, name=name)
            codes, scales = stationary
            for n in range(2):
                cols = slice(n * BANK, (n + 1) * BANK)
                acc = bank[2 * pair + n]
                nc.tensor.matmul_mx(
                    out=acc[:], lhsT=codes[:].bitcast(FP8X4), lhsT_scale=scales[:],
                    rhs=moving[n], rhs_scale=moving_sc[:, cols], start=True, stop=True,
                )
                copies[n](table[:, cols], acc[:])
            return table

        notes_moving = [notes_w[:, n * BANK : (n + 1) * BANK].bitcast(FP8X4) for n in range(2)]
        keys_moving = [keys_w[:, 2 * n * BANK : 2 * (n + 1) * BANK].bitcast(FP4X4) for n in range(2)]
        by_scalar, by_vector = nc.scalar.copy, nc.vector.tensor_copy
        a, b, b_at, r, w, cc = {}, {}, {}, {}, {}, {}

        def score_notes(t, copies):
            b[t] = scores("b_%d" % t, q2_mx[t], notes_moving, notes_sc, t, copies)

        def score_keys(t, copies):
            a[t] = scores("a_%d" % t, q_mx[t], keys_moving, keys_sc, t ^ 2, copies)

        def look_up_notes(t):
            b_at[t] = keep.tile([P, I], F32, name="b_at_%d" % t)
            nc.scalar.activation(b_at[t][:], b[t][:].indirect(idx2[:]), COPY)

        def lead(t):
            r[t] = keep.tile([P, I], F32, name="r_%d" % t)
            nc.vector.tensor_tensor(r[t][:], a[t][:].indirect(idx[:]), b_at[t][:], SUB)

        def pick(t):
            w[t] = keep.tile([P, J], F32, name="w_%d" % t)
            nc.scalar.activation(w[t][:], r[t][:].indirect(idx3[:]), COPY, scale=2.0)

        def place(t):
            nc.vector.tensor_copy(f1[t % F1_TILES][:].indirect(idx4[:]), w[t][:])

        def add_on_gpsimd(t, tag):
            cc[t] = keep.tile([P, T], F32, name="cc_%d" % t, tag=tag)
            nc.gpsimd.tensor_tensor(cc[t][:], a[t][:], f1[t % F1_TILES][:], ADD)

        def add_from_banks(t):
            cc[t] = keep.tile([P, T], F32, name="cc_%d" % t)
            for n in range(2):
                cols = slice(n * BANK, (n + 1) * BANK)
                nc.vector.tensor_tensor(
                    cc[t][:, cols], bank[2 * (t ^ 2) + n][:], f1[t % F1_TILES][:, cols], ADD
                )

        gw = [keep.tile([P, PACK, I_HALF], F32, name="gw_%d" % h) for h in range(2)]
        list_half = I_HALF // LIST_ROWS
        idx5_half = [idx5[:, :list_half], idx5[:, list_half:]]

        def results_on_scalar(t, halves, tag):
            g = keep.tile([P, len(halves), I_HALF], F32, name="g_%d" % t, tag=tag)
            for n, h in enumerate(halves):
                nc.scalar.activation(g[:, n, :], cc[t][:].indirect(idx5_half[h]), COPY)
            for n, h in enumerate(halves):
                nc.scalar.activation(gw[h][:, t, :], g[:, n, :], COPY, scale=rowf_sb[:, t : t + 1])

        def result_on_vector(t, h):
            nc.vector.tensor_tensor(
                gw[h][:, t, :], cc[t][:].indirect(idx5_half[h]), factor[t][:], MULT
            )


        quantise_query2()
        factor = {}
        for t in (2, 3):
            factor[t] = keep.tile([P, I_HALF], F32, name="factor_%d" % t)
            nc.scalar.copy(factor[t][:], rowf_sb[:, t : t + 1].to_broadcast([P, I_HALF]))

        score_notes(0, (by_scalar, by_vector))
        quantise_query_pair(0)
        score_notes(1, (by_scalar, by_scalar))
        for t in (0, 1):
            look_up_notes(t)
        score_keys(0, (by_vector, by_vector))
        score_keys(1, (by_scalar, by_scalar))
        for step in (lead, pick, place):
            for t in (0, 1):
                step(t)
        add_on_gpsimd(0, "cc_0")


        quantise_query_pair(2)
        for t in (2, 3):
            score_notes(t, (by_scalar, by_scalar))
        look_up_notes(2)
        score_keys(2, (by_scalar, by_scalar))
        look_up_notes(3)
        score_keys(3, (by_vector, by_vector))
        for step in (lead, pick, place):
            for t in (2, 3):
                step(t)
        add_on_gpsimd(1, "b_at_3")
        add_on_gpsimd(2, "cc_2")
        add_from_banks(3)


        results_on_scalar(0, (0, 1), "r_3")
        results_on_scalar(1, (0, 1), "g_1")
        result_on_vector(2, 0)
        results_on_scalar(2, (1,), "g_2")
        result_on_vector(3, 0)
        results_on_scalar(3, (1,), "g_1")


        for h in range(2):
            slots = slice(h * I_HALF, (h + 1) * I_HALF)
            gw_bf16 = keep.tile([P, I_HALF * PACK], BF16, name="gw_bf16_%d" % h, align_bytes=64)
            nc.vector.tensor_copy(
                gw_bf16[:].rearrange("p (c i t) -> p c t i", i=LINE, t=PACK),
                gw[h][:].rearrange("p t (c i) -> p c t i", i=LINE),
            )
            gw_codes, gw_scales = quantise(gw_bf16[:], I_HALF, "gw_mx_%d" % h)
            for m in range(E // P):
                chans = slice(m * P, (m + 1) * P)
                acc = bank[4 * h + m][:, :I_HALF]
                nc.tensor.matmul_mx(
                    out=acc, lhsT=mix_w[:, chans].bitcast(FP8X4), lhsT_scale=mix_sc[:, chans],
                    rhs=gw_codes[:].bitcast(FP8X4), rhs_scale=gw_scales[:], start=True, stop=True,
                )
                y = keep.tile([P, I_HALF], F32, name="y_%d_%d" % (h, m))
                copy_out = by_vector if (h, m) == (1, 1) else by_scalar
                copy_out(y[:], acc)
                nc.sync.dma_start(out[chans, slots], y[:])
